import numpy as np
import ml_dtypes


def mxq(x, axis, fmt="e4m3"):
    dtype, down = {"e4m3": (ml_dtypes.float8_e4m3fn, 7), "e5m2": (ml_dtypes.float8_e5m2, 14)}[fmt]
    v = np.moveaxis(np.asarray(x, np.float32).astype(ml_dtypes.bfloat16).astype(np.float64), axis, -1)
    blocks = v.reshape(v.shape[:-1] + (-1, 32))
    amax = np.abs(blocks).max(-1, keepdims=True)
    byte = np.maximum(np.where(amax > 0, np.frexp(amax)[1] - 1 + 127, 0) - down, 1)
    scale = np.exp2(byte - 127.0)
    codes = (blocks / scale).astype(np.float32).astype(dtype).astype(np.float64)
    return np.moveaxis((codes * scale).reshape(v.shape), -1, axis)


WIDE = False


def mx_kscale(k):
    if not WIDE:
        return np.ones(k)
    levels = np.array([10, -10, 5, -5, 0])
    if k % 512:
        return np.exp2(np.random.permutation(np.resize(levels, k // 32))).repeat(32)
    a = np.empty((k // 512, 16))
    for p in range(k // 512):
        a[p, :8] = np.random.permutation(np.resize(levels, 8))
        for g in range(8):
            far = levels[np.abs(levels - a[p, g]) >= 10]
            a[p, g + 8] = far[np.random.randint(len(far))]
    return np.exp2(a.ravel()).repeat(32)


def f64(x):
    return np.asarray(x).astype(np.float64)


def striped(idx):
    return np.tile(np.asarray(idx).reshape(-1, 16).T, (8, 1)).astype(np.uint16)


def unstriped(offs):
    return offs[:16].T.reshape(-1).astype(np.int64)


E2M1 = np.array([0.0, 0.5, 1.0, 1.5, 2.0, 3.0, 4.0, 6.0, -0.0, -0.5, -1.0, -1.5, -2.0, -3.0, -4.0, -6.0])


def pack_weight(w, fmt):
    k, n = w.shape
    w = f64(np.asarray(w, np.float32).astype(ml_dtypes.bfloat16)).reshape(k // 32, 32, n)
    amax = np.abs(w).max(1)
    if fmt == "e4m3":
        byte = np.frexp(amax)[1] - 1 + 127 - 7
    else:
        mant, ex = np.frexp(amax / 6.0)
        byte = np.where(mant > 0.5, ex, ex - 1) + 127
    byte = np.clip(np.where(amax > 0, byte, 1), 1, 254)
    scaled = (w * np.exp2(127.0 - byte)[:, None, :]).reshape(k, n).astype(np.float32)
    by_word = np.ascontiguousarray(scaled.reshape(k // 512, 128, 4, n).transpose(0, 1, 3, 2))
    if fmt == "e4m3":
        words = by_word.astype(ml_dtypes.float8_e4m3fn).view(np.uint8)
    else:
        c = by_word.astype(ml_dtypes.float4_e2m1fn).view(np.uint8) & 0xF
        words = (c[..., 0::2] | (c[..., 1::2] << 4)).reshape(k // 512, 128, 2 * n)
    return np.ascontiguousarray(words), np.ascontiguousarray(byte.astype(np.uint8).reshape(k // 512, 16, n))


def unpack_weight(words, scales, fmt):
    g, _, n = scales.shape
    words = np.ascontiguousarray(words).reshape(g, 128, n, -1)
    if fmt == "e4m3":
        vals = words.view(ml_dtypes.float8_e4m3fn).astype(np.float64)
    else:
        nib = np.empty((g, 128, n, 4), np.uint8)
        nib[..., 0::2] = words & 0xF
        nib[..., 1::2] = words >> 4
        vals = E2M1[nib]
    vals = vals * np.repeat(np.exp2(scales.astype(np.float64) - 127.0), 8, axis=1)[..., None]
    return vals.transpose(0, 1, 3, 2).reshape(g * 512, n)


K, T, J, N = 1024, 2048, 512, 512


def setup_inputs():
    n = np.random.standard_normal
    idx = np.random.permutation(T)[:J]
    fk = mx_kscale(K)
    xtp = pack_weight(n((K, T)) * np.random.uniform(0.3, 1.7, (1, T)) / fk[:, None], "e4m3")
    wbp = pack_weight(n((K, N)) * 1 / np.sqrt(K) * fk[:, None], "e2m1")
    return {
        "xt_words": xtp[0],
        "xt_scales": xtp[1],
        "wa": (n((K, N)) * 1 / np.sqrt(K) * fk[:, None]).astype(np.float32),
        "wb_words": wbp[0],
        "wb_scales": wbp[1],
        "lm": (np.random.uniform(0.4, 1.4, (J, 1))).astype(np.float32),
        "offs": striped(idx),
    }


def reference(xt_words, xt_scales, wa, wb_words, wb_scales, lm, offs):
    idx = unstriped(offs)
    xtu = unpack_weight(xt_words, xt_scales, "e4m3")
    wbu = unpack_weight(wb_words, wb_scales, "e2m1")
    xtidxg = xtu[:, idx]
    waq = mxq(f64(wa), 0, "e4m3")
    a = xtidxg.T @ waq
    b = xtidxg.T @ wbu
    sa = np.minimum(f64(lm) / np.sqrt(np.mean(np.square(a), axis=1, keepdims=True) + 0.01), 1.0)
    sb = np.minimum(f64(lm) / np.sqrt(np.mean(np.square(b), axis=1, keepdims=True) + 0.01), 1.0)
    y = a * sa + 0.5 * b * sb
    return y

@@ -1,0 +1,175 @@
+from contextlib import ExitStack
+
+import concourse.mybir as mybir
+
+K, T, J, N = 1024, 2048, 512, 512
+FLOPS = 2 * 2 * J * K * N
+
+F32 = mybir.dt.float32
+BF16 = mybir.dt.bfloat16
+I32 = mybir.dt.int32
+U32 = mybir.dt.uint32
+U16 = mybir.dt.uint16
+U8 = mybir.dt.uint8
+FP8X4 = mybir.dt.float8_e4m3fn_x4
+FP4X4 = mybir.dt.float4_e2m1fn_x4
+ACT = mybir.ActivationFunctionType
+ALU = mybir.AluOpType
+
+P = 128
+PACK = 4
+PASSES = K // (P * PACK)
+TILES = J // P
+HALF = N // 2
+QUARTER = N // 4
+EPS = 0.01
+B_ON_SCALAR = 4
+
+
+def tile_moe_expert_rows_held_to_size_kernel(tc, xt_words, xt_scales, wa, wb_words, wb_scales, lm, offs, out):
+    nc = tc.nc
+    with ExitStack() as ctx:
+        keep = ctx.enter_context(tc.tile_pool(name="keep", bufs=1))
+        junk = ctx.enter_context(tc.tile_pool(name="junk", bufs=3))
+        psum = ctx.enter_context(tc.psum_pool(name="psum", bufs=1))
+
+        offsets = keep.tile([P, J // 16], U16, name="offsets")
+        nc.sync.dma_start(offsets[:], offs)
+
+        x_scale_win = keep.tile([P, PASSES * T], U8, name="x_scale_win", tag="slot4", align_bytes=64)
+        b_scale = keep.tile([P, PASSES * N], U8, name="b_scale", align_bytes=64)
+        nc.vector.memset(x_scale_win[:].bitcast(I32), 0)
+        nc.gpsimd.memset(b_scale[:].bitcast(I32), 0)
+
+        warm = keep.tile([P, 1], F32, name="warm", tag="slot0", align_bytes=64)
+        warm_out = keep.tile([P, 1], F32, name="warm_out", tag="slot1", align_bytes=64)
+        nc.vector.memset(warm[:], 1.0)
+
+        def load_scale_rows(queue, plane, rows):
+            by_row = rows.rearrange("z (q r) c -> r q z c", r=4)
+            for r in range(4):
+                queue.dma_start(
+                    plane[r:P:32, :].bitcast(I32).rearrange("q (z c) -> q z c", z=PASSES),
+                    by_row[r].bitcast(I32),
+                )
+
+        x_win = [keep.tile([P, T], I32, name=f"x_win{z}", tag=f"slot{2 + z}", align_bytes=64) for z in range(PASSES)]
+        b_words = keep.tile([P, PASSES * 2 * N], U8, name="b_words", align_bytes=64)
+        limit = keep.tile([P, TILES], F32, name="limit")
+
+        def load_x(z):
+            nc.sync.dma_start(x_win[z][:], xt_words[z].rearrange("p t r -> p (t r)").bitcast(I32))
+
+        load_x(0)
+        load_scale_rows(nc.scalar, x_scale_win, xt_scales)
+        nc.scalar.activation(warm_out[:], warm[:], ACT.Abs_reciprocal_sqrt)
+        load_scale_rows(nc.gpsimd, b_scale, wb_scales)
+        nc.sync.dma_start(
+            b_words[:].bitcast(I32).rearrange("p (z c) -> p z c", z=PASSES),
+            wb_words.rearrange("z p c -> p z c").bitcast(I32),
+        )
+        load_x(1)
+        with nc.allow_non_contiguous_dma(reason="one limit a partition"):
+            nc.scalar.dma_start(limit[:], lm.rearrange("(i p) o -> p (i o)", p=P))
+
+        half_limit = keep.tile([P, TILES], F32, name="half_limit")
+        nc.gpsimd.tensor_scalar(half_limit[:], limit[:], 0.5, 0.0, ALU.mult, ALU.add)
+
+        x_scale = [keep.tile([P, J], U8, name=f"x_scale{z}", align_bytes=64) for z in range(PASSES)]
+        for z in range(PASSES):
+            nc.vector.tensor_copy(x_scale[z][:], x_scale_win[:, z * T : (z + 1) * T].indirect(offsets[:]))
+        x_words = [
+            keep.tile([P, J], U32, name=f"x_words{z}", tag=f"slot{4 + z}", align_bytes=64) for z in range(PASSES)
+        ]
+        for z in range(PASSES):
+            for g in range(2):
+                nc.vector.tensor_copy(
+                    x_words[z][:, g * 256 : (g + 1) * 256],
+                    x_win[z][:].bitcast(U32).indirect(offsets[:, g * 16 : (g + 1) * 16]),
+                )
+
+        chunks = [(h, z) for h in range(2) for z in range(PASSES)]
+        a_raw = {}
+        for c, (h, z) in enumerate(chunks):
+            a_raw[h, z] = keep.tile([P, PACK, HALF], F32, name=f"a_raw{h}{z}", tag=f"slot{c}", align_bytes=64)
+            rows = wa[z * P * PACK : (z + 1) * P * PACK, h * HALF : (h + 1) * HALF]
+            nc.sync.dma_start(a_raw[h, z][:], rows.rearrange("(p r) n -> p r n", r=PACK))
+
+        a_bank = [psum.tile([P, N], F32, name=f"a_bank{i}") for i in range(TILES)]
+        b_bank = [psum.tile([P, N], F32, name=f"b_bank{i}") for i in range(TILES)]
+
+        def product(dst, i, z, codes, scales):
+            nc.tensor.matmul_mx(
+                dst,
+                lhsT=x_words[z][:, i * P : (i + 1) * P].bitcast(FP8X4),
+                lhsT_scale=x_scale[z][:, i * P : (i + 1) * P],
+                rhs=codes,
+                rhs_scale=scales,
+                start=(z == 0),
+                stop=(z == PASSES - 1),
+            )
+
+        for g in range(2):
+            for z in range(PASSES):
+                for i in (2 * g, 2 * g + 1):
+                    product(
+                        b_bank[i][:], i, z,
+                        b_words[:, z * 2 * N : (z + 1) * 2 * N].bitcast(FP4X4),
+                        b_scale[:, z * N : (z + 1) * N],
+                    )
+
+        def sum_of_squares(dst, src, width):
+            squares = junk.tile([P, N], F32, name="squares")
+            nc.scalar.activation(squares[:, :width], src, ACT.Square, accum_out=dst)
+
+        b_sumsq = keep.tile([P, TILES], F32, name="b_sumsq")
+        b_rinv = keep.tile([P, TILES], F32, name="b_rinv")
+        b_factor = keep.tile([P, TILES], F32, name="b_factor")
+        b_held = [keep.tile([P, N], F32, name=f"b_held{i}") for i in range(TILES)]
+        for i in range(TILES):
+            col = slice(i, i + 1)
+            sum_of_squares(b_sumsq[:, col], b_bank[i][:], N)
+            nc.scalar.activation(b_rinv[:, col], b_sumsq[:, col], ACT.Abs_reciprocal_sqrt, bias=EPS, scale=1.0 / N)
+            nc.gpsimd.tensor_scalar(b_factor[:, col], b_rinv[:, col], half_limit[:, col], 0.5, ALU.mult, ALU.min)
+
+        def hold_b(i):
+            col = slice(i, i + 1)
+            if i < B_ON_SCALAR:
+                nc.scalar.activation(b_held[i][:], b_bank[i][:], ACT.Copy, scale=b_factor[:, col])
+            else:
+                nc.vector.tensor_scalar(b_held[i][:], b_bank[i][:], b_factor[:, col], None, ALU.mult)
+
+        for i in range(TILES):
+            hold_b(i)
+
+        a_sumsq = keep.tile([P, TILES], F32, name="a_sumsq")
+        a_rinv = keep.tile([P, TILES], F32, name="a_rinv")
+        a_factor = keep.tile([P, TILES], F32, name="a_factor")
+
+        for h, z in chunks:
+            codes = keep.tile([P, HALF], U32, name=f"a_codes{h}{z}", align_bytes=64)
+            scales = keep.tile([P, HALF], U8, name=f"a_scales{h}{z}", align_bytes=64)
+            grouped = []
+            for s in range(2):
+                piece = keep.tile([P, QUARTER * PACK], BF16, name=f"grouped{h}{z}{s}", align_bytes=64)
+                nc.vector.tensor_copy(
+                    piece[:].rearrange("p (c i r) -> p c r i", i=4, r=PACK),
+                    a_raw[h, z][:, :, s * QUARTER : (s + 1) * QUARTER].rearrange("p r (c i) -> p c r i", i=4),
+                )
+                grouped.append(piece)
+            for s in range(2):
+                cols = slice(s * QUARTER, (s + 1) * QUARTER)
+                nc.vector.quantize_mx(out=codes[:, cols].bitcast(FP8X4), scales=scales[:, cols], in_=grouped[s][:])
+            for i in range(TILES):
+                product(a_bank[i][:, h * HALF : (h + 1) * HALF], i, z, codes[:].bitcast(FP8X4), scales[:])
+
+        for i in range(TILES):
+            col = slice(i, i + 1)
+            sum_of_squares(a_sumsq[:, col], a_bank[i][:], N)
+            nc.scalar.activation(a_rinv[:, col], a_sumsq[:, col], ACT.Abs_reciprocal_sqrt, bias=EPS, scale=1.0 / N)
+            nc.gpsimd.tensor_scalar(a_factor[:, col], a_rinv[:, col], limit[:, col], 1.0, ALU.mult, ALU.min)
+            result = keep.tile([P, N], F32, name=f"result{i}")
+            nc.vector.scalar_tensor_tensor(
+                result[:], a_bank[i][:], a_factor[:, col], b_held[i][:], ALU.mult, ALU.add
+            )
+            nc.sync.dma_start(out[i * P : (i + 1) * P, :], result[:])

@@ -1,6 +1,7 @@
 from contextlib import ExitStack
 
 import concourse.mybir as mybir
+from concourse.masks import make_identity
 
 K, T, J, N = 1024, 2048, 512, 512
 FLOPS = 2 * 2 * J * K * N
@@ -23,7 +24,6 @@ TILES = J // P
 HALF = N // 2
 QUARTER = N // 4
 EPS = 0.01
-B_ON_SCALAR = 4
 
 
 def tile_moe_expert_rows_held_to_size_kernel(tc, xt_words, xt_scales, wa, wb_words, wb_scales, lm, offs, out):
@@ -33,17 +33,28 @@ def tile_moe_expert_rows_held_to_size_kernel(tc, xt_words, xt_scales, wa, wb_wor
         junk = ctx.enter_context(tc.tile_pool(name="junk", bufs=3))
         psum = ctx.enter_context(tc.psum_pool(name="psum", bufs=1))
 
-        offsets = keep.tile([P, J // 16], U16, name="offsets")
+        def tile(shape, dtype, name, slot=None):
+            return keep.tile(shape, dtype, name=name, tag=slot or name, align_bytes=64)
+
+        offsets = tile([P, J // 16], U16, "offsets")
         nc.sync.dma_start(offsets[:], offs)
 
-        x_scale_win = keep.tile([P, PASSES * T], U8, name="x_scale_win", tag="slot4", align_bytes=64)
-        b_scale = keep.tile([P, PASSES * N], U8, name="b_scale", align_bytes=64)
+        x_scale_win = tile([P, PASSES * T], U8, "x_scale_win")
         nc.vector.memset(x_scale_win[:].bitcast(I32), 0)
-        nc.gpsimd.memset(b_scale[:].bitcast(I32), 0)
 
-        warm = keep.tile([P, 1], F32, name="warm", tag="slot0", align_bytes=64)
-        warm_out = keep.tile([P, 1], F32, name="warm_out", tag="slot1", align_bytes=64)
-        nc.vector.memset(warm[:], 1.0)
+        limit_rows = tile([P, P], F32, "limit_rows")
+        nc.gpsimd.memset(limit_rows[:], 0.0)
+        nc.scalar.dma_start(limit_rows[0:TILES, :], lm.rearrange("(i p) o -> i (p o)", p=P))
+
+        warm_in = tile([P, 1], F32, "warm_in")
+        warm_bias = tile([P, 1], F32, "warm_bias")
+        warm_out = tile([P, 1], F32, "warm_out")
+        nc.gpsimd.memset(warm_in[:], 1.0)
+        nc.gpsimd.memset(warm_bias[:], 0.0)
+        nc.scalar.activation(warm_out[:], warm_in[:], ACT.Abs_reciprocal_sqrt, bias=warm_bias[:])
+
+        identity = tile([P, P], F32, "identity")
+        make_identity(nc, identity[:])
 
         def load_scale_rows(queue, plane, rows):
             by_row = rows.rearrange("z (q r) c -> r q z c", r=4)
@@ -53,50 +64,68 @@ def tile_moe_expert_rows_held_to_size_kernel(tc, xt_words, xt_scales, wa, wb_wor
                     by_row[r].bitcast(I32),
                 )
 
-        x_win = [keep.tile([P, T], I32, name=f"x_win{z}", tag=f"slot{2 + z}", align_bytes=64) for z in range(PASSES)]
-        b_words = keep.tile([P, PASSES * 2 * N], U8, name="b_words", align_bytes=64)
-        limit = keep.tile([P, TILES], F32, name="limit")
+        x_win = [tile([P, T], I32, "x_win0"), tile([P, T], I32, "x_win1", slot="warm_out")]
+        b_words = tile([P, PASSES * 2 * N], U8, "b_words", slot="warm_in")
+        b_scale = tile([P, PASSES * N], U8, "b_scale", slot="warm_bias")
 
         def load_x(z):
             nc.sync.dma_start(x_win[z][:], xt_words[z].rearrange("p t r -> p (t r)").bitcast(I32))
 
+        chunks = [(h, z) for h in range(2) for z in range(PASSES)]
+        a_raw = {}
+        grouped = {}
+
+        def load_a(chunk, slot):
+            h, z = chunk
+            a_raw[chunk] = tile([P, PACK, HALF], F32, f"a_raw{h}{z}", slot=slot)
+            rows = wa[z * P * PACK : (z + 1) * P * PACK, h * HALF : (h + 1) * HALF]
+            nc.sync.dma_start(a_raw[chunk][:], rows.rearrange("(p r) n -> p r n", r=PACK))
+
+        def cast_a(chunk, copy):
+            h, z = chunk
+            for s in range(2):
+                grouped[h, z, s] = tile([P, QUARTER * PACK], BF16, f"grouped{h}{z}{s}")
+                copy(
+                    grouped[h, z, s][:].rearrange("p (c i r) -> p c r i", i=4, r=PACK),
+                    a_raw[chunk][:, :, s * QUARTER : (s + 1) * QUARTER].rearrange("p r (c i) -> p c r i", i=4),
+                )
+
         load_x(0)
-        load_scale_rows(nc.scalar, x_scale_win, xt_scales)
-        nc.scalar.activation(warm_out[:], warm[:], ACT.Abs_reciprocal_sqrt)
-        load_scale_rows(nc.gpsimd, b_scale, wb_scales)
+        load_scale_rows(nc.sync, x_scale_win, xt_scales)
         nc.sync.dma_start(
             b_words[:].bitcast(I32).rearrange("p (z c) -> p z c", z=PASSES),
             wb_words.rearrange("z p c -> p z c").bitcast(I32),
         )
         load_x(1)
-        with nc.allow_non_contiguous_dma(reason="one limit a partition"):
-            nc.scalar.dma_start(limit[:], lm.rearrange("(i p) o -> p (i o)", p=P))
+        nc.vector.memset(b_scale[:].bitcast(I32), 0)
+        load_scale_rows(nc.scalar, b_scale, wb_scales)
 
-        half_limit = keep.tile([P, TILES], F32, name="half_limit")
-        nc.gpsimd.tensor_scalar(half_limit[:], limit[:], 0.5, 0.0, ALU.mult, ALU.add)
+        a_bank = [psum.tile([P, N], F32, name=f"a_bank{i}") for i in range(TILES)]
+        b_bank = [psum.tile([P, N], F32, name=f"b_bank{i}") for i in range(TILES)]
 
-        x_scale = [keep.tile([P, J], U8, name=f"x_scale{z}", align_bytes=64) for z in range(PASSES)]
-        for z in range(PASSES):
-            nc.vector.tensor_copy(x_scale[z][:], x_scale_win[:, z * T : (z + 1) * T].indirect(offsets[:]))
-        x_words = [
-            keep.tile([P, J], U32, name=f"x_words{z}", tag=f"slot{4 + z}", align_bytes=64) for z in range(PASSES)
-        ]
-        for z in range(PASSES):
+        limit = tile([P, TILES], F32, "limit")
+        half_limit = tile([P, TILES], F32, "half_limit")
+        nc.tensor.transpose(a_bank[TILES - 1][:, :P], limit_rows[:], identity[:])
+        nc.scalar.copy(limit[:], a_bank[TILES - 1][:, :TILES])
+        nc.scalar.activation(half_limit[:], a_bank[TILES - 1][:, :TILES], ACT.Copy, scale=0.5)
+
+        x_scale = [tile([P, J], U8, f"x_scale{z}") for z in range(PASSES)]
+        x_words = [tile([P, J], U32, f"x_words{z}") for z in range(PASSES)]
+
+        def gather_words(z):
             for g in range(2):
                 nc.vector.tensor_copy(
                     x_words[z][:, g * 256 : (g + 1) * 256],
                     x_win[z][:].bitcast(U32).indirect(offsets[:, g * 16 : (g + 1) * 16]),
                 )
 
-        chunks = [(h, z) for h in range(2) for z in range(PASSES)]
-        a_raw = {}
-        for c, (h, z) in enumerate(chunks):
-            a_raw[h, z] = keep.tile([P, PACK, HALF], F32, name=f"a_raw{h}{z}", tag=f"slot{c}", align_bytes=64)
-            rows = wa[z * P * PACK : (z + 1) * P * PACK, h * HALF : (h + 1) * HALF]
-            nc.sync.dma_start(a_raw[h, z][:], rows.rearrange("(p r) n -> p r n", r=PACK))
+        gather_words(0)
+        for z in range(PASSES):
+            nc.vector.tensor_copy(x_scale[z][:], x_scale_win[:, z * T : (z + 1) * T].indirect(offsets[:]))
+        gather_words(1)
 
-        a_bank = [psum.tile([P, N], F32, name=f"a_bank{i}") for i in range(TILES)]
-        b_bank = [psum.tile([P, N], F32, name=f"b_bank{i}") for i in range(TILES)]
+        for chunk, slot in zip(chunks, ("identity", "limit_rows", "x_win0", "x_scale_win")):
+            load_a(chunk, slot)
 
         def product(dst, i, z, codes, scales):
             nc.tensor.matmul_mx(
@@ -118,57 +147,48 @@ def tile_moe_expert_rows_held_to_size_kernel(tc, xt_words, xt_scales, wa, wb_wor
                         b_scale[:, z * N : (z + 1) * N],
                     )
 
-        def sum_of_squares(dst, src, width):
+        def inverse_rms(bank, sumsq, rinv):
             squares = junk.tile([P, N], F32, name="squares")
-            nc.scalar.activation(squares[:, :width], src, ACT.Square, accum_out=dst)
+            nc.scalar.activation(squares[:], bank, ACT.Square, accum_out=sumsq)
+            nc.scalar.activation(rinv, sumsq, ACT.Abs_reciprocal_sqrt, bias=EPS, scale=1.0 / N)
 
-        b_sumsq = keep.tile([P, TILES], F32, name="b_sumsq")
-        b_rinv = keep.tile([P, TILES], F32, name="b_rinv")
-        b_factor = keep.tile([P, TILES], F32, name="b_factor")
-        b_held = [keep.tile([P, N], F32, name=f"b_held{i}") for i in range(TILES)]
+        b_sumsq = tile([P, TILES], F32, "b_sumsq")
+        b_rinv = tile([P, TILES], F32, "b_rinv")
+        b_held = [tile([P, N], F32, f"b_held{i}") for i in range(TILES)]
         for i in range(TILES):
-            col = slice(i, i + 1)
-            sum_of_squares(b_sumsq[:, col], b_bank[i][:], N)
-            nc.scalar.activation(b_rinv[:, col], b_sumsq[:, col], ACT.Abs_reciprocal_sqrt, bias=EPS, scale=1.0 / N)
-            nc.gpsimd.tensor_scalar(b_factor[:, col], b_rinv[:, col], half_limit[:, col], 0.5, ALU.mult, ALU.min)
+            inverse_rms(b_bank[i][:], b_sumsq[:, i : i + 1], b_rinv[:, i : i + 1])
 
-        def hold_b(i):
+        def hold_b(i, slot):
             col = slice(i, i + 1)
-            if i < B_ON_SCALAR:
-                nc.scalar.activation(b_held[i][:], b_bank[i][:], ACT.Copy, scale=b_factor[:, col])
+            factor = tile([P, 1], F32, f"b_factor{i}", slot=slot)
+            nc.vector.tensor_scalar(factor[:], b_rinv[:, col], half_limit[:, col], 0.5, ALU.mult, ALU.min)
+            if i < TILES - 1:
+                nc.scalar.activation(b_held[i][:], b_bank[i][:], ACT.Copy, scale=factor[:])
             else:
-                nc.vector.tensor_scalar(b_held[i][:], b_bank[i][:], b_factor[:, col], None, ALU.mult)
+                nc.vector.tensor_scalar(b_held[i][:], b_bank[i][:], factor[:], None, ALU.mult)
 
-        for i in range(TILES):
-            hold_b(i)
-
-        a_sumsq = keep.tile([P, TILES], F32, name="a_sumsq")
-        a_rinv = keep.tile([P, TILES], F32, name="a_rinv")
-        a_factor = keep.tile([P, TILES], F32, name="a_factor")
+        held_after = {(0, 1): (0, 1), (1, 0): (2,), (1, 1): (3,)}
 
         for h, z in chunks:
-            codes = keep.tile([P, HALF], U32, name=f"a_codes{h}{z}", align_bytes=64)
-            scales = keep.tile([P, HALF], U8, name=f"a_scales{h}{z}", align_bytes=64)
-            grouped = []
-            for s in range(2):
-                piece = keep.tile([P, QUARTER * PACK], BF16, name=f"grouped{h}{z}{s}", align_bytes=64)
-                nc.vector.tensor_copy(
-                    piece[:].rearrange("p (c i r) -> p c r i", i=4, r=PACK),
-                    a_raw[h, z][:, :, s * QUARTER : (s + 1) * QUARTER].rearrange("p r (c i) -> p c r i", i=4),
-                )
-                grouped.append(piece)
+            codes = tile([P, HALF], U32, f"a_codes{h}{z}")
+            scales = tile([P, HALF], U8, f"a_scales{h}{z}")
+            cast_a((h, z), nc.vector.tensor_copy)
             for s in range(2):
                 cols = slice(s * QUARTER, (s + 1) * QUARTER)
-                nc.vector.quantize_mx(out=codes[:, cols].bitcast(FP8X4), scales=scales[:, cols], in_=grouped[s][:])
+                nc.vector.quantize_mx(out=codes[:, cols].bitcast(FP8X4), scales=scales[:, cols], in_=grouped[h, z, s][:])
             for i in range(TILES):
                 product(a_bank[i][:, h * HALF : (h + 1) * HALF], i, z, codes[:].bitcast(FP8X4), scales[:])
+            for s, i in enumerate(held_after.get((h, z), ())):
+                hold_b(i, f"grouped{h}{z}{1 - s}")
 
+        a_sumsq = tile([P, TILES], F32, "a_sumsq")
+        a_rinv = tile([P, TILES], F32, "a_rinv")
+        a_factor = tile([P, TILES], F32, "a_factor")
         for i in range(TILES):
             col = slice(i, i + 1)
-            sum_of_squares(a_sumsq[:, col], a_bank[i][:], N)
-            nc.scalar.activation(a_rinv[:, col], a_sumsq[:, col], ACT.Abs_reciprocal_sqrt, bias=EPS, scale=1.0 / N)
-            nc.gpsimd.tensor_scalar(a_factor[:, col], a_rinv[:, col], limit[:, col], 1.0, ALU.mult, ALU.min)
-            result = keep.tile([P, N], F32, name=f"result{i}")
+            inverse_rms(a_bank[i][:], a_sumsq[:, col], a_rinv[:, col])
+            nc.vector.tensor_scalar(a_factor[:, col], a_rinv[:, col], limit[:, col], 1.0, ALU.mult, ALU.min)
+            result = tile([P, N], F32, f"result{i}")
             nc.vector.scalar_tensor_tensor(
                 result[:], a_bank[i][:], a_factor[:, col], b_held[i][:], ALU.mult, ALU.add
             )

@@ -42,16 +42,16 @@ def tile_moe_expert_rows_held_to_size_kernel(tc, xt_words, xt_scales, wa, wb_wor
         x_scale_win = tile([P, PASSES * T], U8, "x_scale_win")
         nc.vector.memset(x_scale_win[:].bitcast(I32), 0)
 
-        limit_rows = tile([P, P], F32, "limit_rows")
-        nc.gpsimd.memset(limit_rows[:], 0.0)
-        nc.scalar.dma_start(limit_rows[0:TILES, :], lm.rearrange("(i p) o -> i (p o)", p=P))
-
         warm_in = tile([P, 1], F32, "warm_in")
         warm_bias = tile([P, 1], F32, "warm_bias")
         warm_out = tile([P, 1], F32, "warm_out")
         nc.gpsimd.memset(warm_in[:], 1.0)
         nc.gpsimd.memset(warm_bias[:], 0.0)
         nc.scalar.activation(warm_out[:], warm_in[:], ACT.Abs_reciprocal_sqrt, bias=warm_bias[:])
+
+        limit_rows = tile([P, P], F32, "limit_rows")
+        nc.gpsimd.memset(limit_rows[:], 0.0)
+        nc.sync.dma_start(limit_rows[0:TILES, :], lm.rearrange("(i p) o -> i (p o)", p=P))
 
         identity = tile([P, P], F32, "identity")
         make_identity(nc, identity[:])
@@ -64,9 +64,9 @@ def tile_moe_expert_rows_held_to_size_kernel(tc, xt_words, xt_scales, wa, wb_wor
                     by_row[r].bitcast(I32),
                 )
 
-        x_win = [tile([P, T], I32, "x_win0"), tile([P, T], I32, "x_win1", slot="warm_out")]
-        b_words = tile([P, PASSES * 2 * N], U8, "b_words", slot="warm_in")
-        b_scale = tile([P, PASSES * N], U8, "b_scale", slot="warm_bias")
+        x_win = [tile([P, T], I32, "x_win0"), tile([P, T], I32, "x_win1", slot="warm_in")]
+        b_words = tile([P, PASSES * 2 * N], U8, "b_words", slot="warm_bias")
+        b_scale = tile([P, PASSES * N], U8, "b_scale", slot="warm_out")
 
         def load_x(z):
             nc.sync.dma_start(x_win[z][:], xt_words[z].rearrange("p t r -> p (t r)").bitcast(I32))
@@ -92,13 +92,13 @@ def tile_moe_expert_rows_held_to_size_kernel(tc, xt_words, xt_scales, wa, wb_wor
 
         load_x(0)
         load_scale_rows(nc.sync, x_scale_win, xt_scales)
+        load_x(1)
         nc.sync.dma_start(
             b_words[:].bitcast(I32).rearrange("p (z c) -> p z c", z=PASSES),
             wb_words.rearrange("z p c -> p z c").bitcast(I32),
         )
-        load_x(1)
         nc.vector.memset(b_scale[:].bitcast(I32), 0)
-        load_scale_rows(nc.scalar, b_scale, wb_scales)
+        load_scale_rows(nc.sync, b_scale, wb_scales)
 
         a_bank = [psum.tile([P, N], F32, name=f"a_bank{i}") for i in range(TILES)]
         b_bank = [psum.tile([P, N], F32, name=f"b_bank{i}") for i in range(TILES)]
@@ -127,6 +127,8 @@ def tile_moe_expert_rows_held_to_size_kernel(tc, xt_words, xt_scales, wa, wb_wor
         for chunk, slot in zip(chunks, ("identity", "limit_rows", "x_win0", "x_scale_win")):
             load_a(chunk, slot)
 
+        cast_a(chunks[0], nc.scalar.copy)
+
         def product(dst, i, z, codes, scales):
             nc.tensor.matmul_mx(
                 dst,
@@ -152,34 +154,44 @@ def tile_moe_expert_rows_held_to_size_kernel(tc, xt_words, xt_scales, wa, wb_wor
             nc.scalar.activation(squares[:], bank, ACT.Square, accum_out=sumsq)
             nc.scalar.activation(rinv, sumsq, ACT.Abs_reciprocal_sqrt, bias=EPS, scale=1.0 / N)
 
-        b_sumsq = tile([P, TILES], F32, "b_sumsq")
+        b_sumsq = tile([P, TILES], F32, "b_sumsq", slot="identity")
         b_rinv = tile([P, TILES], F32, "b_rinv")
         b_held = [tile([P, N], F32, f"b_held{i}") for i in range(TILES)]
         for i in range(TILES):
             inverse_rms(b_bank[i][:], b_sumsq[:, i : i + 1], b_rinv[:, i : i + 1])
 
-        def hold_b(i, slot):
-            col = slice(i, i + 1)
-            factor = tile([P, 1], F32, f"b_factor{i}", slot=slot)
-            nc.vector.tensor_scalar(factor[:], b_rinv[:, col], half_limit[:, col], 0.5, ALU.mult, ALU.min)
-            if i < TILES - 1:
-                nc.scalar.activation(b_held[i][:], b_bank[i][:], ACT.Copy, scale=factor[:])
-            else:
-                nc.vector.tensor_scalar(b_held[i][:], b_bank[i][:], factor[:], None, ALU.mult)
+        b_factor = {}
 
-        held_after = {(0, 1): (0, 1), (1, 0): (2,), (1, 1): (3,)}
+        def b_factors(tiles, slot):
+            factors = tile([P, len(tiles)], F32, f"b_factor{tiles[0]}", slot=slot)
+            for e, i in enumerate(tiles):
+                col = slice(i, i + 1)
+                b_factor[i] = factors[:, e : e + 1]
+                nc.vector.tensor_scalar(b_factor[i], b_rinv[:, col], half_limit[:, col], 0.5, ALU.mult, ALU.min)
+
+        def hold_b(i, on_scalar):
+            if on_scalar:
+                nc.scalar.activation(b_held[i][:], b_bank[i][:], ACT.Copy, scale=b_factor[i])
+            else:
+                nc.vector.tensor_scalar(b_held[i][:], b_bank[i][:], b_factor[i], None, ALU.mult)
 
         for h, z in chunks:
             codes = tile([P, HALF], U32, f"a_codes{h}{z}")
             scales = tile([P, HALF], U8, f"a_scales{h}{z}")
-            cast_a((h, z), nc.vector.tensor_copy)
+            if (h, z) != chunks[0]:
+                cast_a((h, z), nc.vector.tensor_copy)
             for s in range(2):
                 cols = slice(s * QUARTER, (s + 1) * QUARTER)
                 nc.vector.quantize_mx(out=codes[:, cols].bitcast(FP8X4), scales=scales[:, cols], in_=grouped[h, z, s][:])
             for i in range(TILES):
                 product(a_bank[i][:, h * HALF : (h + 1) * HALF], i, z, codes[:].bitcast(FP8X4), scales[:])
-            for s, i in enumerate(held_after.get((h, z), ())):
-                hold_b(i, f"grouped{h}{z}{1 - s}")
+            if (h, z) == chunks[2]:
+                b_factors((0,), "grouped101")
+                hold_b(0, on_scalar=True)
+
+        b_factors((1, 2, 3), "grouped111")
+        hold_b(1, on_scalar=False)
+        hold_b(2, on_scalar=False)
 
         a_sumsq = tile([P, TILES], F32, "a_sumsq")
         a_rinv = tile([P, TILES], F32, "a_rinv")
@@ -187,9 +199,14 @@ def tile_moe_expert_rows_held_to_size_kernel(tc, xt_words, xt_scales, wa, wb_wor
         for i in range(TILES):
             col = slice(i, i + 1)
             inverse_rms(a_bank[i][:], a_sumsq[:, col], a_rinv[:, col])
-            nc.vector.tensor_scalar(a_factor[:, col], a_rinv[:, col], limit[:, col], 1.0, ALU.mult, ALU.min)
+            nc.gpsimd.tensor_scalar(a_factor[:, col], a_rinv[:, col], limit[:, col], 1.0, ALU.mult, ALU.min)
+            if i == TILES - 1:
+                hold_b(i, on_scalar=True)
             result = tile([P, N], F32, f"result{i}")
-            nc.vector.scalar_tensor_tensor(
-                result[:], a_bank[i][:], a_factor[:, col], b_held[i][:], ALU.mult, ALU.add
-            )
-            nc.sync.dma_start(out[i * P : (i + 1) * P, :], result[:])
+            width = HALF if i == TILES - 1 else N
+            for n0 in range(0, N, width):
+                cols = slice(n0, n0 + width)
+                nc.vector.scalar_tensor_tensor(
+                    result[:, cols], a_bank[i][:, cols], a_factor[:, col], b_held[i][:, cols], ALU.mult, ALU.add
+                )
+                nc.sync.dma_start(out[i * P : (i + 1) * P, cols], result[:, cols])

from contextlib import ExitStack

import concourse.mybir as mybir
from concourse.masks import make_identity

K, T, J, N = 1024, 2048, 512, 512
FLOPS = 2 * 2 * J * K * N

F32 = mybir.dt.float32
BF16 = mybir.dt.bfloat16
I32 = mybir.dt.int32
U32 = mybir.dt.uint32
U16 = mybir.dt.uint16
U8 = mybir.dt.uint8
FP8X4 = mybir.dt.float8_e4m3fn_x4
FP4X4 = mybir.dt.float4_e2m1fn_x4
ACT = mybir.ActivationFunctionType
ALU = mybir.AluOpType

P = 128
PACK = 4
PASSES = K // (P * PACK)
TILES = J // P
HALF = N // 2
QUARTER = N // 4
EPS = 0.01


def tile_moe_expert_rows_held_to_size_kernel(tc, xt_words, xt_scales, wa, wb_words, wb_scales, lm, offs, out):
    nc = tc.nc
    with ExitStack() as ctx:
        keep = ctx.enter_context(tc.tile_pool(name="keep", bufs=1))
        junk = ctx.enter_context(tc.tile_pool(name="junk", bufs=3))
        psum = ctx.enter_context(tc.psum_pool(name="psum", bufs=1))

        def tile(shape, dtype, name, slot=None):
            return keep.tile(shape, dtype, name=name, tag=slot or name, align_bytes=64)

        offsets = tile([P, J // 16], U16, "offsets")
        nc.sync.dma_start(offsets[:], offs)

        x_scale_win = tile([P, PASSES * T], U8, "x_scale_win")
        nc.vector.memset(x_scale_win[:].bitcast(I32), 0)

        warm_in = tile([P, 1], F32, "warm_in")
        warm_bias = tile([P, 1], F32, "warm_bias")
        warm_out = tile([P, 1], F32, "warm_out")
        nc.gpsimd.memset(warm_in[:], 1.0)
        nc.gpsimd.memset(warm_bias[:], 0.0)
        nc.scalar.activation(warm_out[:], warm_in[:], ACT.Abs_reciprocal_sqrt, bias=warm_bias[:])

        limit_rows = tile([P, P], F32, "limit_rows")
        nc.gpsimd.memset(limit_rows[:], 0.0)
        nc.sync.dma_start(limit_rows[0:TILES, :], lm.rearrange("(i p) o -> i (p o)", p=P))

        identity = tile([P, P], F32, "identity")
        make_identity(nc, identity[:])

        def load_scale_rows(queue, plane, rows):
            by_row = rows.rearrange("z (q r) c -> r q z c", r=4)
            for r in range(4):
                queue.dma_start(
                    plane[r:P:32, :].bitcast(I32).rearrange("q (z c) -> q z c", z=PASSES),
                    by_row[r].bitcast(I32),
                )

        x_win = [tile([P, T], I32, "x_win0"), tile([P, T], I32, "x_win1", slot="warm_in")]
        b_words = tile([P, PASSES * 2 * N], U8, "b_words", slot="warm_bias")
        b_scale = tile([P, PASSES * N], U8, "b_scale", slot="warm_out")

        def load_x(z):
            nc.sync.dma_start(x_win[z][:], xt_words[z].rearrange("p t r -> p (t r)").bitcast(I32))

        chunks = [(h, z) for h in range(2) for z in range(PASSES)]
        a_raw = {}
        grouped = {}

        def load_a(chunk, slot):
            h, z = chunk
            a_raw[chunk] = tile([P, PACK, HALF], F32, f"a_raw{h}{z}", slot=slot)
            rows = wa[z * P * PACK : (z + 1) * P * PACK, h * HALF : (h + 1) * HALF]
            nc.sync.dma_start(a_raw[chunk][:], rows.rearrange("(p r) n -> p r n", r=PACK))

        def cast_a(chunk, copy):
            h, z = chunk
            for s in range(2):
                grouped[h, z, s] = tile([P, QUARTER * PACK], BF16, f"grouped{h}{z}{s}")
                copy(
                    grouped[h, z, s][:].rearrange("p (c i r) -> p c r i", i=4, r=PACK),
                    a_raw[chunk][:, :, s * QUARTER : (s + 1) * QUARTER].rearrange("p r (c i) -> p c r i", i=4),
                )

        load_x(0)
        load_scale_rows(nc.sync, x_scale_win, xt_scales)
        load_x(1)
        nc.sync.dma_start(
            b_words[:].bitcast(I32).rearrange("p (z c) -> p z c", z=PASSES),
            wb_words.rearrange("z p c -> p z c").bitcast(I32),
        )
        nc.vector.memset(b_scale[:].bitcast(I32), 0)
        load_scale_rows(nc.sync, b_scale, wb_scales)

        a_bank = [psum.tile([P, N], F32, name=f"a_bank{i}") for i in range(TILES)]
        b_bank = [psum.tile([P, N], F32, name=f"b_bank{i}") for i in range(TILES)]

        limit = tile([P, TILES], F32, "limit")
        half_limit = tile([P, TILES], F32, "half_limit")
        nc.tensor.transpose(a_bank[TILES - 1][:, :P], limit_rows[:], identity[:])
        nc.scalar.copy(limit[:], a_bank[TILES - 1][:, :TILES])
        nc.scalar.activation(half_limit[:], a_bank[TILES - 1][:, :TILES], ACT.Copy, scale=0.5)

        x_scale = [tile([P, J], U8, f"x_scale{z}") for z in range(PASSES)]
        x_words = [tile([P, J], U32, f"x_words{z}") for z in range(PASSES)]

        def gather_words(z):
            for g in range(2):
                nc.vector.tensor_copy(
                    x_words[z][:, g * 256 : (g + 1) * 256],
                    x_win[z][:].bitcast(U32).indirect(offsets[:, g * 16 : (g + 1) * 16]),
                )

        gather_words(0)
        for z in range(PASSES):
            nc.vector.tensor_copy(x_scale[z][:], x_scale_win[:, z * T : (z + 1) * T].indirect(offsets[:]))
        gather_words(1)

        for chunk, slot in zip(chunks, ("identity", "limit_rows", "x_win0", "x_scale_win")):
            load_a(chunk, slot)

        cast_a(chunks[0], nc.scalar.copy)

        def product(dst, i, z, codes, scales):
            nc.tensor.matmul_mx(
                dst,
                lhsT=x_words[z][:, i * P : (i + 1) * P].bitcast(FP8X4),
                lhsT_scale=x_scale[z][:, i * P : (i + 1) * P],
                rhs=codes,
                rhs_scale=scales,
                start=(z == 0),
                stop=(z == PASSES - 1),
            )

        for g in range(2):
            for z in range(PASSES):
                for i in (2 * g, 2 * g + 1):
                    product(
                        b_bank[i][:], i, z,
                        b_words[:, z * 2 * N : (z + 1) * 2 * N].bitcast(FP4X4),
                        b_scale[:, z * N : (z + 1) * N],
                    )

        def inverse_rms(bank, sumsq, rinv):
            squares = junk.tile([P, N], F32, name="squares")
            nc.scalar.activation(squares[:], bank, ACT.Square, accum_out=sumsq)
            nc.scalar.activation(rinv, sumsq, ACT.Abs_reciprocal_sqrt, bias=EPS, scale=1.0 / N)

        b_sumsq = tile([P, TILES], F32, "b_sumsq", slot="identity")
        b_rinv = tile([P, TILES], F32, "b_rinv")
        b_held = [tile([P, N], F32, f"b_held{i}") for i in range(TILES)]
        for i in range(TILES):
            inverse_rms(b_bank[i][:], b_sumsq[:, i : i + 1], b_rinv[:, i : i + 1])

        b_factor = {}

        def b_factors(tiles, slot):
            factors = tile([P, len(tiles)], F32, f"b_factor{tiles[0]}", slot=slot)
            for e, i in enumerate(tiles):
                col = slice(i, i + 1)
                b_factor[i] = factors[:, e : e + 1]
                nc.vector.tensor_scalar(b_factor[i], b_rinv[:, col], half_limit[:, col], 0.5, ALU.mult, ALU.min)

        def hold_b(i, on_scalar):
            if on_scalar:
                nc.scalar.activation(b_held[i][:], b_bank[i][:], ACT.Copy, scale=b_factor[i])
            else:
                nc.vector.tensor_scalar(b_held[i][:], b_bank[i][:], b_factor[i], None, ALU.mult)

        for h, z in chunks:
            codes = tile([P, HALF], U32, f"a_codes{h}{z}")
            scales = tile([P, HALF], U8, f"a_scales{h}{z}")
            if (h, z) != chunks[0]:
                cast_a((h, z), nc.vector.tensor_copy)
            for s in range(2):
                cols = slice(s * QUARTER, (s + 1) * QUARTER)
                nc.vector.quantize_mx(out=codes[:, cols].bitcast(FP8X4), scales=scales[:, cols], in_=grouped[h, z, s][:])
            for i in range(TILES):
                product(a_bank[i][:, h * HALF : (h + 1) * HALF], i, z, codes[:].bitcast(FP8X4), scales[:])
            if (h, z) == chunks[2]:
                b_factors((0,), "grouped101")
                hold_b(0, on_scalar=True)

        b_factors((1, 2, 3), "grouped111")
        hold_b(1, on_scalar=False)
        hold_b(2, on_scalar=False)

        a_sumsq = tile([P, TILES], F32, "a_sumsq")
        a_rinv = tile([P, TILES], F32, "a_rinv")
        a_factor = tile([P, TILES], F32, "a_factor")
        for i in range(TILES):
            col = slice(i, i + 1)
            inverse_rms(a_bank[i][:], a_sumsq[:, col], a_rinv[:, col])
            nc.gpsimd.tensor_scalar(a_factor[:, col], a_rinv[:, col], limit[:, col], 1.0, ALU.mult, ALU.min)
            if i == TILES - 1:
                hold_b(i, on_scalar=True)
            result = tile([P, N], F32, f"result{i}")
            width = HALF if i == TILES - 1 else N
            for n0 in range(0, N, width):
                cols = slice(n0, n0 + width)
                nc.vector.scalar_tensor_tensor(
                    result[:, cols], a_bank[i][:, cols], a_factor[:, col], b_held[i][:, cols], ALU.mult, ALU.add
                )
                nc.sync.dma_start(out[i * P : (i + 1) * P, cols], result[:, cols])
